import numpy as np
import ml_dtypes


def mxq(x, axis, fmt="e4m3"):
    dtype, down = {"e4m3": (ml_dtypes.float8_e4m3fn, 7), "e5m2": (ml_dtypes.float8_e5m2, 14)}[fmt]
    v = np.moveaxis(np.asarray(x, np.float32).astype(ml_dtypes.bfloat16).astype(np.float64), axis, -1)
    blocks = v.reshape(v.shape[:-1] + (-1, 32))
    amax = np.abs(blocks).max(-1, keepdims=True)
    byte = np.maximum(np.where(amax > 0, np.frexp(amax)[1] - 1 + 127, 0) - down, 1)
    scale = np.exp2(byte - 127.0)
    codes = (blocks / scale).astype(np.float32).astype(dtype).astype(np.float64)
    return np.moveaxis((codes * scale).reshape(v.shape), -1, axis)


WIDE = False


def mx_kscale(k):
    if not WIDE:
        return np.ones(k)
    levels = np.array([10, -10, 5, -5, 0])
    if k % 512:
        return np.exp2(np.random.permutation(np.resize(levels, k // 32))).repeat(32)
    a = np.empty((k // 512, 16))
    for p in range(k // 512):
        a[p, :8] = np.random.permutation(np.resize(levels, 8))
        for g in range(8):
            far = levels[np.abs(levels - a[p, g]) >= 10]
            a[p, g + 8] = far[np.random.randint(len(far))]
    return np.exp2(a.ravel()).repeat(32)


def f64(x):
    return np.asarray(x).astype(np.float64)


def striped(idx):
    return np.tile(idx.reshape(-1, 16).T, (8, 1)).astype(np.uint16)


def unstriped(offs):
    return offs[:16].T.reshape(-1).astype(np.int64)


E2M1 = np.array([0.0, 0.5, 1.0, 1.5, 2.0, 3.0, 4.0, 6.0, -0.0, -0.5, -1.0, -1.5, -2.0, -3.0, -4.0, -6.0])


def pack_weight(w, fmt):
    k, n = w.shape
    w = f64(np.asarray(w, np.float32).astype(ml_dtypes.bfloat16)).reshape(k // 32, 32, n)
    amax = np.abs(w).max(1)
    if fmt == "e4m3":
        byte = np.frexp(amax)[1] - 1 + 127 - 7
    else:
        mant, ex = np.frexp(amax / 6.0)
        byte = np.where(mant > 0.5, ex, ex - 1) + 127
    byte = np.clip(np.where(amax > 0, byte, 1), 1, 254)
    scaled = (w * np.exp2(127.0 - byte)[:, None, :]).reshape(k, n).astype(np.float32)
    by_word = np.ascontiguousarray(scaled.reshape(k // 512, 128, 4, n).transpose(0, 1, 3, 2))
    if fmt == "e4m3":
        words = by_word.astype(ml_dtypes.float8_e4m3fn).view(np.uint8)
    else:
        c = by_word.astype(ml_dtypes.float4_e2m1fn).view(np.uint8) & 0xF
        words = (c[..., 0::2] | (c[..., 1::2] << 4)).reshape(k // 512, 128, 2 * n)
    return np.ascontiguousarray(words), np.ascontiguousarray(byte.astype(np.uint8).reshape(k // 512, 16, n))


def unpack_weight(words, scales, fmt):
    g, _, n = scales.shape
    words = np.ascontiguousarray(words).reshape(g, 128, n, -1)
    if fmt == "e4m3":
        vals = words.view(ml_dtypes.float8_e4m3fn).astype(np.float64)
    else:
        nib = np.empty((g, 128, n, 4), np.uint8)
        nib[..., 0::2] = words & 0xF
        nib[..., 1::2] = words >> 4
        vals = E2M1[nib]
    vals = vals * np.repeat(np.exp2(scales.astype(np.float64) - 127.0), 8, axis=1)[..., None]
    return vals.transpose(0, 1, 3, 2).reshape(g * 512, n)


def relu(v):
    return np.maximum(v, 0.0)


K, T, E, C, N = 1024, 1024, 8, 256, 128
K8 = 512


def by_expert(wq, xq):
    return np.concatenate([wq[e].T @ xq[:, e * C:(e + 1) * C] for e in range(E)], axis=1)


def setup_inputs():
    n = np.random.standard_normal
    s = mx_kscale(K)[:, None]
    first = np.random.permutation(np.repeat(np.arange(E), T // E))
    second = (first + 1 + np.random.permutation(np.repeat(np.arange(E - 1), -(-T // (E - 1)))[:T])) % E
    while np.bincount(second, minlength=E).max() != T // E:
        load = np.bincount(second, minlength=E); hi, lo = int(load.argmax()), int(load.argmin())
        t = np.flatnonzero((second == hi) & (first != lo))[0]; second[t] = lo
    slot_token = np.empty(E * C, np.int64); pos = np.empty((2, T), np.int64); fill = np.zeros(E, np.int64)
    place = np.stack([np.random.permutation(C) for _ in range(E)])
    for r, deal in enumerate((first, second)):
        for t in np.random.permutation(T):
            e = deal[t]; j = e * C + place[e, fill[e]]; fill[e] += 1; slot_token[j] = t; pos[r, t] = j
    g = np.random.uniform(0.2, 0.8, T)
    w = n((E, K, N)) / np.sqrt(K) / s[None]
    w8 = [pack_weight(m[:K8], "e4m3") for m in w]
    w4 = [pack_weight(m[K8:], "e2m1") for m in w]
    return {
        "xT": (n((K, T)) * s).astype(np.float32),
        "w8_words": np.stack([m[0] for m in w8]),
        "w8_scales": np.stack([m[1] for m in w8]),
        "w4_words": np.stack([m[0] for m in w4]),
        "w4_scales": np.stack([m[1] for m in w4]),
        "b": (0.3 * n((N, E))).astype(np.float32),
        "gate": np.stack([np.tile(g, (N, 1)), np.tile(1.0 - g, (N, 1))]).astype(np.float32),
        "offs": striped(slot_token),
        "pos1": striped(pos[0]),
        "pos2": striped(pos[1]),
    }


def reference(xT, w8_words, w8_scales, w4_words, w4_scales, b, gate, offs, pos1, pos2):
    idx = unstriped(offs)
    w = np.stack([np.concatenate([unpack_weight(w8_words[e], w8_scales[e], "e4m3"), unpack_weight(w4_words[e], w4_scales[e], "e2m1")]) for e in range(E)])
    xq = mxq(f64(xT)[:, idx], 0, "e4m3")
    y = by_expert(w, xq)
    y = relu(y + np.repeat(f64(b), C, axis=1))
    return f64(gate[0]) * y[:, unstriped(pos1)] + f64(gate[1]) * y[:, unstriped(pos2)]

@@ -1,0 +1,154 @@
+from contextlib import ExitStack
+
+import concourse.mybir as mybir
+
+K, T, E, C, N = 1024, 1024, 8, 256, 128
+SLOTS = E * C
+FLOPS = 2 * SLOTS * K * N
+
+F32 = mybir.dt.float32
+BF16 = mybir.dt.bfloat16
+I32 = mybir.dt.int32
+U32 = mybir.dt.uint32
+U16 = mybir.dt.uint16
+U8 = mybir.dt.uint8
+FP8X4 = mybir.dt.float8_e4m3fn_x4
+FP4X4 = mybir.dt.float4_e2m1fn_x4
+COPY = mybir.ActivationFunctionType.Copy
+RELU = mybir.ActivationFunctionType.Relu
+MULT = mybir.AluOpType.mult
+
+P = 128
+PASSES = 2
+FIRST_ROW = (4, 0)
+CHUNKS = ((0, 512), (512, 768), (768, 1024))
+VECTOR_SHARE = 0.625
+HALF = 128
+
+
+def tile_moe_pln_lin_relu_kernel(
+    tc, xT, w8_words, w8_scales, w4_words, w4_scales, b, gate, offs, pos1, pos2, out
+):
+    nc = tc.nc
+    with ExitStack() as ctx:
+        keep = ctx.enter_context(tc.tile_pool(name="keep", bufs=1))
+        psum = ctx.enter_context(tc.psum_pool(name="psum", bufs=1))
+
+        offs_sb = keep.tile([P, SLOTS // 16], U16, name="offs_sb")
+        pos1_sb = keep.tile([P, T // 16], U16, name="pos1_sb")
+        pos2_sb = keep.tile([P, T // 16], U16, name="pos2_sb")
+        w8_sb = keep.tile([P, E, 4 * N], U8, name="w8_sb", align_bytes=64)
+        w4_sb = keep.tile([P, E, 2 * N], U8, name="w4_sb", align_bytes=64)
+        w_scales = keep.tile([P, E * N], U8, name="w_scales", align_bytes=64)
+        x_scales = keep.tile([P, T], U8, name="x_scales", align_bytes=64)
+        slot_scales = keep.tile([P, SLOTS], U8, name="slot_scales", align_bytes=64)
+        x_codes = [keep.tile([P, T], U32, name=f"x_codes{a}", align_bytes=64) for a in range(PASSES)]
+        slot_codes = [keep.tile([P, SLOTS], U32, name=f"slot_codes{a}", align_bytes=64) for a in range(PASSES)]
+        bias = keep.tile([P, E], F32, name="bias")
+        gates = keep.tile([P, 2, T], F32, name="gates")
+        y = keep.tile([P, SLOTS], F32, name="y")
+        warm = keep.tile([P, 8], F32, name="warm")
+
+        nc.gpsimd.memset(warm[:], 0.0)
+        nc.scalar.activation(warm[:, 0:1], warm[:, 1:2], RELU)
+        nc.gpsimd.memset(x_scales[:], 0)
+        nc.gpsimd.memset(w_scales[:].bitcast(I32), 0)
+
+        raw = {}
+        for a in range(PASSES):
+            for lo, hi in CHUNKS:
+                raw[a, lo] = keep.tile([P, 4, hi - lo], F32, name=f"raw{a}_{lo}")
+                nc.sync.dma_start(
+                    raw[a, lo][:],
+                    xT[512 * a : 512 * (a + 1), lo:hi].rearrange("(p j) t -> p j t", j=4),
+                )
+            if a == 0:
+                nc.sync.dma_start(offs_sb[:], offs)
+        nc.sync.dma_start(w8_sb[:].bitcast(I32), w8_words[:, 0].rearrange("e p n r -> p e (n r)").bitcast(I32))
+        nc.sync.dma_start(w4_sb[:].bitcast(I32), w4_words[:, 0].rearrange("e p m -> p e m").bitcast(I32))
+        for source, first in ((w8_scales, FIRST_ROW[0]), (w4_scales, FIRST_ROW[1])):
+            for q in range(4):
+                nc.sync.dma_start(
+                    w_scales[32 * q + first : 32 * q + first + 4, :].bitcast(I32).rearrange("q (e n) -> q e n", e=E),
+                    source[:, 0, 4 * q : 4 * q + 4, :].rearrange("e q n -> q e n").bitcast(I32),
+                )
+        nc.sync.dma_start(bias[:], b)
+        nc.sync.dma_start(pos1_sb[:], pos1)
+        nc.sync.dma_start(pos2_sb[:], pos2)
+        nc.sync.dma_start(gates[:], gate.rearrange("g n t -> n g t"))
+
+        grouped = {}
+
+        def cast(a, lo, hi, vector_share):
+            width = hi - lo
+            grouped[a, lo] = keep.tile([P, width, 4], BF16, name=f"grouped{a}_{lo}", align_bytes=64)
+            v = int(width * vector_share)
+            src = raw[a, lo][:].rearrange("p j t -> p t j")
+            if v:
+                nc.vector.tensor_copy(grouped[a, lo][:, 0:v, :], src[:, 0:v, :])
+            if v < width:
+                nc.scalar.activation(grouped[a, lo][:, v:width, :], src[:, v:width, :], COPY)
+
+        def quantize(a, lo, hi):
+            nc.vector.quantize_mx(
+                out=x_codes[a][:, lo:hi].bitcast(FP8X4),
+                scales=x_scales[FIRST_ROW[a] : P, lo:hi],
+                in_=grouped[a, lo][:].rearrange("p t j -> p (t j)"),
+            )
+
+        def gather_codes(a, lo, hi):
+            nc.vector.tensor_copy(slot_codes[a][:, lo:hi], x_codes[a][:].indirect(offs_sb[:, lo // 16 : hi // 16]))
+
+        def gather_scales(lo, hi):
+            nc.vector.tensor_copy(slot_scales[:, lo:hi], x_scales[:].indirect(offs_sb[:, lo // 16 : hi // 16]))
+
+        banks = []
+
+        def multiply(lo, hi):
+            e = lo // C
+            acc = psum.tile([P, C], F32, name=f"acc{len(banks) % 8}")
+            banks.append(acc)
+            for s in range(lo, hi, HALF):
+                cols = slice(s - lo, s - lo + HALF)
+                for a in range(PASSES):
+                    weights = w8_sb[:, e, :].bitcast(FP8X4) if a == 0 else w4_sb[:, e, :].bitcast(FP4X4)
+                    nc.tensor.matmul_mx(
+                        out=acc[:, cols],
+                        lhsT=weights,
+                        lhsT_scale=w_scales[FIRST_ROW[a] : P, e * N : (e + 1) * N],
+                        rhs=slot_codes[a][:, s : s + HALF].bitcast(FP8X4),
+                        rhs_scale=slot_scales[FIRST_ROW[a] : P, s : s + HALF],
+                        start=(a == 0),
+                        stop=(a == PASSES - 1),
+                    )
+            nc.scalar.activation(y[:, lo:hi], acc[:, 0 : hi - lo], RELU, bias=bias[:, e : e + 1])
+
+        for lo, hi in CHUNKS:
+            cast(0, lo, hi, VECTOR_SHARE)
+            quantize(0, lo, hi)
+        gather_codes(0, 0, 768)
+        gather_codes(0, 768, 1536)
+        for lo, hi in CHUNKS:
+            cast(1, lo, hi, 0.0)
+            quantize(1, lo, hi)
+        gather_codes(0, 1536, 2048)
+        for lo, hi in ((0, 768), (768, 1536)):
+            gather_scales(lo, hi)
+            gather_codes(1, lo, hi)
+            for s in range(lo, hi, C):
+                multiply(s, s + C)
+        gather_scales(1536, 2048)
+        gather_codes(1, 1536, 1920)
+        multiply(1536, 1792)
+        multiply(1792, 1920)
+        gather_codes(1, 1920, 2048)
+        multiply(1920, 2048)
+
+        for lo, hi in ((0, 512), (512, 768), (768, 1024)):
+            first = keep.tile([P, hi - lo], F32, name=f"first{lo}")
+            second = keep.tile([P, hi - lo], F32, name=f"second{lo}")
+            result = keep.tile([P, hi - lo], F32, name=f"result{lo}")
+            nc.vector.tensor_tensor(first[:], y[:].indirect(pos1_sb[:, lo // 16 : hi // 16]), gates[:, 0, lo:hi], MULT)
+            nc.vector.tensor_tensor(second[:], y[:].indirect(pos2_sb[:, lo // 16 : hi // 16]), gates[:, 1, lo:hi], MULT)
+            nc.vector.tensor_add(result[:], first[:], second[:])
+            nc.sync.dma_start(out[:, lo:hi], result[:])

@@ -17,12 +17,14 @@ FP4X4 = mybir.dt.float4_e2m1fn_x4
 COPY = mybir.ActivationFunctionType.Copy
 RELU = mybir.ActivationFunctionType.Relu
 MULT = mybir.AluOpType.mult
+ADD = mybir.AluOpType.add
+MAX = mybir.AluOpType.max
 
 P = 128
 PASSES = 2
 FIRST_ROW = (4, 0)
 CHUNKS = ((0, 512), (512, 768), (768, 1024))
-VECTOR_SHARE = 0.625
+VECTOR_SHARE = 0.6875
 HALF = 128
 
 
@@ -121,7 +123,10 @@ def tile_moe_pln_lin_relu_kernel(
                         start=(a == 0),
                         stop=(a == PASSES - 1),
                     )
-            nc.scalar.activation(y[:, lo:hi], acc[:, 0 : hi - lo], RELU, bias=bias[:, e : e + 1])
+            if hi == SLOTS:
+                nc.vector.tensor_scalar(y[:, lo:hi], acc[:, 0 : hi - lo], bias[:, e : e + 1], 0.0, ADD, MAX)
+            else:
+                nc.scalar.activation(y[:, lo:hi], acc[:, 0 : hi - lo], RELU, bias=bias[:, e : e + 1])
 
         for lo, hi in CHUNKS:
             cast(0, lo, hi, VECTOR_SHARE)
@@ -130,8 +135,11 @@ def tile_moe_pln_lin_relu_kernel(
         gather_codes(0, 768, 1536)
         for lo, hi in CHUNKS:
             cast(1, lo, hi, 0.0)
-            quantize(1, lo, hi)
-        gather_codes(0, 1536, 2048)
+        quantize(1, *CHUNKS[0])
+        quantize(1, *CHUNKS[1])
+        gather_codes(0, 1536, 1920)
+        quantize(1, *CHUNKS[2])
+        gather_codes(0, 1920, 2048)
         for lo, hi in ((0, 768), (768, 1536)):
             gather_scales(lo, hi)
             gather_codes(1, lo, hi)
@@ -144,11 +152,23 @@ def tile_moe_pln_lin_relu_kernel(
         gather_codes(1, 1920, 2048)
         multiply(1920, 2048)
 
-        for lo, hi in ((0, 512), (512, 768), (768, 1024)):
-            first = keep.tile([P, hi - lo], F32, name=f"first{lo}")
-            second = keep.tile([P, hi - lo], F32, name=f"second{lo}")
-            result = keep.tile([P, hi - lo], F32, name=f"result{lo}")
-            nc.vector.tensor_tensor(first[:], y[:].indirect(pos1_sb[:, lo // 16 : hi // 16]), gates[:, 0, lo:hi], MULT)
-            nc.vector.tensor_tensor(second[:], y[:].indirect(pos2_sb[:, lo // 16 : hi // 16]), gates[:, 1, lo:hi], MULT)
-            nc.vector.tensor_add(result[:], first[:], second[:])
-            nc.sync.dma_start(out[:, lo:hi], result[:])
+        first = keep.tile([P, T], F32, name="first")
+        second = keep.tile([P, T], F32, name="second")
+        result = keep.tile([P, T], F32, name="result")
+
+        def second_choice(lo, hi):
+            nc.vector.tensor_tensor(
+                second[:, lo:hi], y[:].indirect(pos2_sb[:, lo // 16 : hi // 16]), gates[:, 1, lo:hi], MULT
+            )
+
+        def add_and_store(lo, hi):
+            nc.vector.tensor_add(result[:, lo:hi], first[:, lo:hi], second[:, lo:hi])
+            nc.sync.dma_start(out[:, lo:hi], result[:, lo:hi])
+
+        nc.vector.tensor_tensor(first[:], y[:].indirect(pos1_sb[:]), gates[:, 0, :], MULT)
+        second_choice(0, 512)
+        second_choice(512, 768)
+        add_and_store(0, 512)
+        second_choice(768, 1024)
+        add_and_store(512, 768)
+        add_and_store(768, 1024)

@@ -24,6 +24,7 @@ P = 128
 PASSES = 2
 FIRST_ROW = (4, 0)
 CHUNKS = ((0, 512), (512, 768), (768, 1024))
+LOADS = (CHUNKS, ((0, 256), (256, 512), (512, 768), (768, 1024)))
 VECTOR_SHARE = 0.6875
 HALF = 128
 
@@ -58,7 +59,7 @@ def tile_moe_pln_lin_relu_kernel(
 
         raw = {}
         for a in range(PASSES):
-            for lo, hi in CHUNKS:
+            for lo, hi in LOADS[a]:
                 raw[a, lo] = keep.tile([P, 4, hi - lo], F32, name=f"raw{a}_{lo}")
                 nc.sync.dma_start(
                     raw[a, lo][:],
@@ -79,23 +80,29 @@ def tile_moe_pln_lin_relu_kernel(
         nc.sync.dma_start(pos2_sb[:], pos2)
         nc.sync.dma_start(gates[:], gate.rearrange("g n t -> n g t"))
 
-        grouped = {}
+        grouped = [keep.tile([P, T, 4], BF16, name=f"grouped{a}", align_bytes=64) for a in range(PASSES)]
+
+        def interleave(copy, a, lo, hi, first):
+            copy(
+                grouped[a][:, lo:hi, :].rearrange("p (c i) j -> p c j i", i=4),
+                raw[a, first][:, :, lo - first : hi - first].rearrange("p j (c i) -> p c j i", i=4),
+            )
+
+        def scalar_copy(dst, src):
+            nc.scalar.activation(dst, src, COPY)
 
         def cast(a, lo, hi, vector_share):
-            width = hi - lo
-            grouped[a, lo] = keep.tile([P, width, 4], BF16, name=f"grouped{a}_{lo}", align_bytes=64)
-            v = int(width * vector_share)
-            src = raw[a, lo][:].rearrange("p j t -> p t j")
-            if v:
-                nc.vector.tensor_copy(grouped[a, lo][:, 0:v, :], src[:, 0:v, :])
-            if v < width:
-                nc.scalar.activation(grouped[a, lo][:, v:width, :], src[:, v:width, :], COPY)
+            v = lo + int((hi - lo) * vector_share)
+            if v > lo:
+                interleave(nc.vector.tensor_copy, a, lo, v, lo)
+            if v < hi:
+                interleave(scalar_copy, a, v, hi, lo)
 
         def quantize(a, lo, hi):
             nc.vector.quantize_mx(
                 out=x_codes[a][:, lo:hi].bitcast(FP8X4),
                 scales=x_scales[FIRST_ROW[a] : P, lo:hi],
-                in_=grouped[a, lo][:].rearrange("p t j -> p (t j)"),
+                in_=grouped[a][:, lo:hi, :].rearrange("p t j -> p (t j)"),
             )
 
         def gather_codes(a, lo, hi):
@@ -133,7 +140,7 @@ def tile_moe_pln_lin_relu_kernel(
             quantize(0, lo, hi)
         gather_codes(0, 0, 768)
         gather_codes(0, 768, 1536)
-        for lo, hi in CHUNKS:
+        for lo, hi in LOADS[1]:
             cast(1, lo, hi, 0.0)
         quantize(1, *CHUNKS[0])
         quantize(1, *CHUNKS[1])

@@ -23,8 +23,10 @@ MAX = mybir.AluOpType.max
 P = 128
 PASSES = 2
 FIRST_ROW = (4, 0)
-CHUNKS = ((0, 512), (512, 768), (768, 1024))
-LOADS = (CHUNKS, ((0, 256), (256, 512), (512, 768), (768, 1024)))
+LOADS = (
+    ((0, 512), (512, 768), (768, 896), (896, 1024)),
+    ((0, 256), (256, 512), (512, 768), (768, 896), (896, 1024)),
+)
 VECTOR_SHARE = 0.6875
 HALF = 128
 
@@ -135,17 +137,18 @@ def tile_moe_pln_lin_relu_kernel(
             else:
                 nc.scalar.activation(y[:, lo:hi], acc[:, 0 : hi - lo], RELU, bias=bias[:, e : e + 1])
 
-        for lo, hi in CHUNKS:
-            cast(0, lo, hi, VECTOR_SHARE)
+        for lo, hi in LOADS[0]:
+            cast(0, lo, hi, 0.5 if lo == 0 else VECTOR_SHARE)
             quantize(0, lo, hi)
         gather_codes(0, 0, 768)
         gather_codes(0, 768, 1536)
         for lo, hi in LOADS[1]:
             cast(1, lo, hi, 0.0)
-        quantize(1, *CHUNKS[0])
-        quantize(1, *CHUNKS[1])
+        quantize(1, 0, 512)
         gather_codes(0, 1536, 1920)
-        quantize(1, *CHUNKS[2])
+        quantize(1, 512, 768)
+        quantize(1, 768, 896)
+        quantize(1, 896, 1024)
         gather_codes(0, 1920, 2048)
         for lo, hi in ((0, 768), (768, 1536)):
             gather_scales(lo, hi)

from contextlib import ExitStack

import concourse.mybir as mybir

K, T, E, C, N = 1024, 1024, 8, 256, 128
SLOTS = E * C
FLOPS = 2 * SLOTS * K * N

F32 = mybir.dt.float32
BF16 = mybir.dt.bfloat16
I32 = mybir.dt.int32
U32 = mybir.dt.uint32
U16 = mybir.dt.uint16
U8 = mybir.dt.uint8
FP8X4 = mybir.dt.float8_e4m3fn_x4
FP4X4 = mybir.dt.float4_e2m1fn_x4
COPY = mybir.ActivationFunctionType.Copy
RELU = mybir.ActivationFunctionType.Relu
MULT = mybir.AluOpType.mult
ADD = mybir.AluOpType.add
MAX = mybir.AluOpType.max

P = 128
PASSES = 2
FIRST_ROW = (4, 0)
LOADS = (
    ((0, 512), (512, 768), (768, 896), (896, 1024)),
    ((0, 256), (256, 512), (512, 768), (768, 896), (896, 1024)),
)
VECTOR_SHARE = 0.6875
HALF = 128


def tile_moe_pln_lin_relu_kernel(
    tc, xT, w8_words, w8_scales, w4_words, w4_scales, b, gate, offs, pos1, pos2, out
):
    nc = tc.nc
    with ExitStack() as ctx:
        keep = ctx.enter_context(tc.tile_pool(name="keep", bufs=1))
        psum = ctx.enter_context(tc.psum_pool(name="psum", bufs=1))

        offs_sb = keep.tile([P, SLOTS // 16], U16, name="offs_sb")
        pos1_sb = keep.tile([P, T // 16], U16, name="pos1_sb")
        pos2_sb = keep.tile([P, T // 16], U16, name="pos2_sb")
        w8_sb = keep.tile([P, E, 4 * N], U8, name="w8_sb", align_bytes=64)
        w4_sb = keep.tile([P, E, 2 * N], U8, name="w4_sb", align_bytes=64)
        w_scales = keep.tile([P, E * N], U8, name="w_scales", align_bytes=64)
        x_scales = keep.tile([P, T], U8, name="x_scales", align_bytes=64)
        slot_scales = keep.tile([P, SLOTS], U8, name="slot_scales", align_bytes=64)
        x_codes = [keep.tile([P, T], U32, name=f"x_codes{a}", align_bytes=64) for a in range(PASSES)]
        slot_codes = [keep.tile([P, SLOTS], U32, name=f"slot_codes{a}", align_bytes=64) for a in range(PASSES)]
        bias = keep.tile([P, E], F32, name="bias")
        gates = keep.tile([P, 2, T], F32, name="gates")
        y = keep.tile([P, SLOTS], F32, name="y")
        warm = keep.tile([P, 8], F32, name="warm")

        nc.gpsimd.memset(warm[:], 0.0)
        nc.scalar.activation(warm[:, 0:1], warm[:, 1:2], RELU)
        nc.gpsimd.memset(x_scales[:], 0)
        nc.gpsimd.memset(w_scales[:].bitcast(I32), 0)

        raw = {}
        for a in range(PASSES):
            for lo, hi in LOADS[a]:
                raw[a, lo] = keep.tile([P, 4, hi - lo], F32, name=f"raw{a}_{lo}")
                nc.sync.dma_start(
                    raw[a, lo][:],
                    xT[512 * a : 512 * (a + 1), lo:hi].rearrange("(p j) t -> p j t", j=4),
                )
            if a == 0:
                nc.sync.dma_start(offs_sb[:], offs)
        nc.sync.dma_start(w8_sb[:].bitcast(I32), w8_words[:, 0].rearrange("e p n r -> p e (n r)").bitcast(I32))
        nc.sync.dma_start(w4_sb[:].bitcast(I32), w4_words[:, 0].rearrange("e p m -> p e m").bitcast(I32))
        for source, first in ((w8_scales, FIRST_ROW[0]), (w4_scales, FIRST_ROW[1])):
            for q in range(4):
                nc.sync.dma_start(
                    w_scales[32 * q + first : 32 * q + first + 4, :].bitcast(I32).rearrange("q (e n) -> q e n", e=E),
                    source[:, 0, 4 * q : 4 * q + 4, :].rearrange("e q n -> q e n").bitcast(I32),
                )
        nc.sync.dma_start(bias[:], b)
        nc.sync.dma_start(pos1_sb[:], pos1)
        nc.sync.dma_start(pos2_sb[:], pos2)
        nc.sync.dma_start(gates[:], gate.rearrange("g n t -> n g t"))

        grouped = [keep.tile([P, T, 4], BF16, name=f"grouped{a}", align_bytes=64) for a in range(PASSES)]

        def interleave(copy, a, lo, hi, first):
            copy(
                grouped[a][:, lo:hi, :].rearrange("p (c i) j -> p c j i", i=4),
                raw[a, first][:, :, lo - first : hi - first].rearrange("p j (c i) -> p c j i", i=4),
            )

        def scalar_copy(dst, src):
            nc.scalar.activation(dst, src, COPY)

        def cast(a, lo, hi, vector_share):
            v = lo + int((hi - lo) * vector_share)
            if v > lo:
                interleave(nc.vector.tensor_copy, a, lo, v, lo)
            if v < hi:
                interleave(scalar_copy, a, v, hi, lo)

        def quantize(a, lo, hi):
            nc.vector.quantize_mx(
                out=x_codes[a][:, lo:hi].bitcast(FP8X4),
                scales=x_scales[FIRST_ROW[a] : P, lo:hi],
                in_=grouped[a][:, lo:hi, :].rearrange("p t j -> p (t j)"),
            )

        def gather_codes(a, lo, hi):
            nc.vector.tensor_copy(slot_codes[a][:, lo:hi], x_codes[a][:].indirect(offs_sb[:, lo // 16 : hi // 16]))

        def gather_scales(lo, hi):
            nc.vector.tensor_copy(slot_scales[:, lo:hi], x_scales[:].indirect(offs_sb[:, lo // 16 : hi // 16]))

        banks = []

        def multiply(lo, hi):
            e = lo // C
            acc = psum.tile([P, C], F32, name=f"acc{len(banks) % 8}")
            banks.append(acc)
            for s in range(lo, hi, HALF):
                cols = slice(s - lo, s - lo + HALF)
                for a in range(PASSES):
                    weights = w8_sb[:, e, :].bitcast(FP8X4) if a == 0 else w4_sb[:, e, :].bitcast(FP4X4)
                    nc.tensor.matmul_mx(
                        out=acc[:, cols],
                        lhsT=weights,
                        lhsT_scale=w_scales[FIRST_ROW[a] : P, e * N : (e + 1) * N],
                        rhs=slot_codes[a][:, s : s + HALF].bitcast(FP8X4),
                        rhs_scale=slot_scales[FIRST_ROW[a] : P, s : s + HALF],
                        start=(a == 0),
                        stop=(a == PASSES - 1),
                    )
            if hi == SLOTS:
                nc.vector.tensor_scalar(y[:, lo:hi], acc[:, 0 : hi - lo], bias[:, e : e + 1], 0.0, ADD, MAX)
            else:
                nc.scalar.activation(y[:, lo:hi], acc[:, 0 : hi - lo], RELU, bias=bias[:, e : e + 1])

        for lo, hi in LOADS[0]:
            cast(0, lo, hi, 0.5 if lo == 0 else VECTOR_SHARE)
            quantize(0, lo, hi)
        gather_codes(0, 0, 768)
        gather_codes(0, 768, 1536)
        for lo, hi in LOADS[1]:
            cast(1, lo, hi, 0.0)
        quantize(1, 0, 512)
        gather_codes(0, 1536, 1920)
        quantize(1, 512, 768)
        quantize(1, 768, 896)
        quantize(1, 896, 1024)
        gather_codes(0, 1920, 2048)
        for lo, hi in ((0, 768), (768, 1536)):
            gather_scales(lo, hi)
            gather_codes(1, lo, hi)
            for s in range(lo, hi, C):
                multiply(s, s + C)
        gather_scales(1536, 2048)
        gather_codes(1, 1536, 1920)
        multiply(1536, 1792)
        multiply(1792, 1920)
        gather_codes(1, 1920, 2048)
        multiply(1920, 2048)

        first = keep.tile([P, T], F32, name="first")
        second = keep.tile([P, T], F32, name="second")
        result = keep.tile([P, T], F32, name="result")

        def second_choice(lo, hi):
            nc.vector.tensor_tensor(
                second[:, lo:hi], y[:].indirect(pos2_sb[:, lo // 16 : hi // 16]), gates[:, 1, lo:hi], MULT
            )

        def add_and_store(lo, hi):
            nc.vector.tensor_add(result[:, lo:hi], first[:, lo:hi], second[:, lo:hi])
            nc.sync.dma_start(out[:, lo:hi], result[:, lo:hi])

        nc.vector.tensor_tensor(first[:], y[:].indirect(pos1_sb[:]), gates[:, 0, :], MULT)
        second_choice(0, 512)
        second_choice(512, 768)
        add_and_store(0, 512)
        second_choice(768, 1024)
        add_and_store(512, 768)
        add_and_store(768, 1024)
